import numpy as np
import ml_dtypes


def mxq(x, axis, fmt="e4m3"):
    dtype, down = {"e4m3": (ml_dtypes.float8_e4m3fn, 7), "e5m2": (ml_dtypes.float8_e5m2, 14)}[fmt]
    v = np.moveaxis(np.asarray(x, np.float32).astype(ml_dtypes.bfloat16).astype(np.float64), axis, -1)
    blocks = v.reshape(v.shape[:-1] + (-1, 32))
    amax = np.abs(blocks).max(-1, keepdims=True)
    byte = np.maximum(np.where(amax > 0, np.frexp(amax)[1] - 1 + 127, 0) - down, 1)
    scale = np.exp2(byte - 127.0)
    codes = (blocks / scale).astype(np.float32).astype(dtype).astype(np.float64)
    return np.moveaxis((codes * scale).reshape(v.shape), -1, axis)


WIDE = False


def mx_kscale(k):
    if not WIDE:
        return np.ones(k)
    levels = np.array([10, -10, 5, -5, 0])
    if k % 512:
        return np.exp2(np.random.permutation(np.resize(levels, k // 32))).repeat(32)
    a = np.empty((k // 512, 16))
    for p in range(k // 512):
        a[p, :8] = np.random.permutation(np.resize(levels, 8))
        for g in range(8):
            far = levels[np.abs(levels - a[p, g]) >= 10]
            a[p, g + 8] = far[np.random.randint(len(far))]
    return np.exp2(a.ravel()).repeat(32)


def f64(x):
    return np.asarray(x).astype(np.float64)


def striped(idx):
    return np.tile(idx.reshape(-1, 16).T, (8, 1)).astype(np.uint16)


def unstriped(offs):
    return offs[:16].T.reshape(-1).astype(np.int64)


def pack_weight(w):
    k, n = w.shape
    w = f64(np.asarray(w, np.float32).astype(ml_dtypes.bfloat16)).reshape(k // 32, 32, n)
    amax = np.abs(w).max(1)
    byte = np.clip(np.where(amax > 0, np.frexp(amax)[1] - 1 + 127 - 7, 1), 1, 254)
    scaled = (w * np.exp2(127.0 - byte)[:, None, :]).reshape(k, n).astype(np.float32)
    words = np.ascontiguousarray(scaled.reshape(k // 512, 128, 4, n).transpose(0, 1, 3, 2)).astype(ml_dtypes.float8_e4m3fn).view(np.uint8)
    return words, np.ascontiguousarray(byte.astype(np.uint8).reshape(k // 512, 16, n))


def unpack_weight(words, scales):
    g, p, n, _ = words.shape
    vals = np.ascontiguousarray(words).view(ml_dtypes.float8_e4m3fn).astype(np.float64) * np.repeat(np.exp2(scales.astype(np.float64) - 127.0), 8, axis=1)[..., None]
    return vals.transpose(0, 1, 3, 2).reshape(g * 512, n)


K, T, S, N, U = 512, 1024, 512, 128, 512
P = 2 ** 7


def setup_inputs():
    n = np.random.standard_normal
    s = mx_kscale(K)[:, None]
    packed_xT = pack_weight(n((K, T)) * s)
    return {
        "x_words": packed_xT[0],
        "x_scales": packed_xT[1],
        "w1": (n((K, N)) / np.sqrt(K) / s).astype(np.float32),
        "one": (np.tile(np.random.uniform(0.85, 1.0, S), (P, 1))).astype(np.float32),
        "alpha": (np.random.uniform(0.3, 1.5, (N, 1))).astype(np.float32),
        "offs": striped(np.random.permutation(T)[:S]),
        "up": striped(np.random.randint(0, S, U)),
        "lo": striped(np.random.randint(0, S, U)),
    }


def reference(x_words, x_scales, w1, one, alpha, offs, up, lo):
    xq = unpack_weight(x_words, x_scales)[:, unstriped(offs)]
    y = mxq(f64(w1), 0, "e4m3").T @ xq
    suc = np.log(np.exp(y) + 1.0) + 0.1
    sat = f64(one)[:1] / (np.sqrt(f64(alpha) * ((suc) ** 2) + 1.0))
    cond = np.sqrt(sat) * ((-1.0 * (np.sqrt(-1.0 * ((sat) ** 2) + 1.001)) + 1.0) ** 2)
    ku = cond[:, unstriped(up)]
    kl = cond[:, unstriped(lo)]
    kf = np.sqrt(ku * kl)
    return 4.0 * (kf * (suc[:, unstriped(lo)] - suc[:, unstriped(up)] + 1.0))

@@ -1,0 +1,136 @@
+import math
+from contextlib import ExitStack
+
+import concourse.mybir as mybir
+from concourse.masks import make_identity
+
+K, T, S, N, U = 512, 1024, 512, 128, 512
+FLOPS = 2 * K * S * N
+
+F32 = mybir.dt.float32
+BF16 = mybir.dt.bfloat16
+I32 = mybir.dt.int32
+U32 = mybir.dt.uint32
+U16 = mybir.dt.uint16
+U8 = mybir.dt.uint8
+FP8X4 = mybir.dt.float8_e4m3fn_x4
+ALU = mybir.AluOpType
+ACT = mybir.ActivationFunctionType
+
+P = 128
+HALF = S // 2
+
+
+def tile_picked_yrich_geo_p_kernel(tc, x_words, x_scales, w1, one, alpha, offs, up, lo, out):
+    nc = tc.nc
+    halves = [slice(0, HALF), slice(HALF, S)]
+    list_halves = [slice(0, HALF // 16), slice(HALF // 16, S // 16)]
+    with ExitStack() as ctx:
+        sb = ctx.enter_context(tc.tile_pool(name="sb", bufs=1))
+        ps = ctx.enter_context(tc.psum_pool(name="ps", bufs=1))
+
+        offs_t = sb.tile([P, S // 16], U16)
+        up_t = sb.tile([P, U // 16], U16)
+        lo_t = sb.tile([P, U // 16], U16)
+        words = sb.tile([P, T], U32)
+        scales = sb.tile([P, T], U8)
+        w_raw = sb.tile([P, 4, N], F32)
+        one_col = sb.tile([P, 4], F32)
+        alpha_col = sb.tile([P, 1], F32)
+
+        nc.vector.memset(scales[:].bitcast(I32), 0)
+        nc.sync.dma_start(offs_t[:], offs)
+        for q in range(4):
+            nc.sync.dma_start(scales[32 * q : 32 * q + 4, :].bitcast(I32), x_scales[0, 4 * q : 4 * q + 4, :].bitcast(I32))
+        nc.sync.dma_start(words[:].bitcast(I32), x_words[0].rearrange("p n t -> p (n t)").bitcast(I32))
+        nc.gpsimd.dma_start(w_raw[:], w1.rearrange("(p j) n -> p j n", j=4))
+        nc.gpsimd.dma_start(alpha_col[:], alpha)
+        nc.gpsimd.dma_start(one_col[:], one[0, :].rearrange("(p j) -> p j", j=4))
+        nc.sync.dma_start(up_t[:], up)
+        nc.sync.dma_start(lo_t[:], lo)
+
+        ident = sb.tile([P, P], F32)
+        make_identity(nc, ident[:])
+        half_t = sb.tile([P, 1], F32)
+        nc.gpsimd.memset(half_t[:], 0.5)
+        root_alpha = sb.tile([P, 1], F32)
+        nc.gpsimd.tensor_tensor(root_alpha[:], alpha_col[:], half_t[:], ALU.pow)
+        root_alpha_tenth = sb.tile([P, 1], F32)
+        nc.gpsimd.tensor_scalar(root_alpha_tenth[:], root_alpha[:], 0.1, 0.0, ALU.mult, ALU.add)
+
+        w_bf = sb.tile([P, N, 4], BF16, align_bytes=64)
+        nc.scalar.copy(w_bf[:], w_raw[:].rearrange("p j n -> p n j"))
+        w_codes = sb.tile([P, N], U32, align_bytes=64)
+        w_scales = sb.tile([P, N], U8, align_bytes=64)
+        x_codes = sb.tile([P, S], U32, align_bytes=64)
+        x_sc = sb.tile([P, S], U8, align_bytes=64)
+        nc.vector.tensor_copy(x_codes[:, halves[0]], words[:].indirect(offs_t[:, list_halves[0]]))
+        nc.vector.tensor_copy(x_sc[:, halves[0]], scales[:].indirect(offs_t[:, list_halves[0]]))
+        nc.vector.quantize_mx(out=w_codes[:].bitcast(FP8X4), scales=w_scales[:], in_=w_bf[:].rearrange("p n j -> p (n j)"))
+        nc.vector.tensor_copy(x_codes[:, halves[1]], words[:].indirect(offs_t[:, list_halves[1]]))
+        nc.vector.tensor_copy(x_sc[:, halves[1]], scales[:].indirect(offs_t[:, list_halves[1]]))
+
+        win = sb.tile([P, 4 * S], F32)
+        soft = win[:, 0:S]
+        inv_sat2 = win[:, S : 2 * S]
+        expy = win[:, 2 * S : 3 * S]
+        zz = win[:, 2 * S : 3 * S]
+        one_plus = win[:, 3 * S : 4 * S]
+
+        y = [ps.tile([P, HALF], F32, name=f"y{h}") for h in range(2)]
+        for h in range(2):
+            nc.tensor.matmul_mx(out=y[h][:], lhsT=w_codes[:].bitcast(FP8X4), lhsT_scale=w_scales[:],
+                                rhs=x_codes[:, halves[h]].bitcast(FP8X4), rhs_scale=x_sc[:, halves[h]],
+                                start=True, stop=True)
+            nc.scalar.activation(expy[:, halves[h]], y[h][:], ACT.Exp)
+        nc.vector.tensor_scalar(one_plus, expy, 2.0**60, 1.0, ALU.min, ALU.add)
+
+        inv_one = sb.tile([P, 4], F32)
+        nc.vector.reciprocal(inv_one[:], one_col[:])
+        inv_one2 = sb.tile([P, 4], F32)
+        nc.vector.tensor_tensor(inv_one2[:], inv_one[:], inv_one[:], ALU.mult)
+        k2 = ps.tile([P, 4, P], F32)
+        for j in range(4):
+            nc.tensor.transpose(k2[:, j, :], inv_one2[:, j : j + 1].to_broadcast([P, P]), ident[:])
+        k2_cells = k2[:].rearrange("p j c -> p c j")
+
+        lg = sb.tile([P, S], F32)
+        sq = sb.tile([P, S], F32)
+        ln_u = sb.tile([P, S], F32)
+        ln_v = sb.tile([P, S], F32)
+        for h in range(2):
+            nc.scalar.activation(lg[:, halves[h]], one_plus[:, halves[h]], ACT.Ln)
+            nc.vector.tensor_tensor(soft[:, halves[h]], y[h][:], lg[:, halves[h]], ALU.max)
+        for h in range(2):
+            nc.scalar.activation(sq[:, halves[h]], soft[:, halves[h]], ACT.Square, scale=root_alpha[:], bias=root_alpha_tenth[:])
+            nc.vector.scalar_tensor_tensor(inv_sat2[:, halves[h]].rearrange("p (c j) -> p c j", j=4),
+                                           sq[:, halves[h]].rearrange("p (c j) -> p c j", j=4), 1.0,
+                                           k2_cells[:, 64 * h : 64 * h + 64, :], ALU.add, ALU.mult)
+        for h in range(2):
+            nc.scalar.activation(ln_v[:, halves[h]], inv_sat2[:, halves[h]], ACT.Ln, scale=1.001, bias=-1.0)
+            nc.scalar.activation(ln_u[:, halves[h]], inv_sat2[:, halves[h]], ACT.Ln)
+
+        neg_up = sb.tile([P, U], F32)
+        nc.vector.tensor_scalar(neg_up[:], win[:].indirect(up_t[:]), -1.0, 1.0, ALU.mult, ALU.add)
+        nc.vector.scalar_tensor_tensor(zz, ln_v[:], -0.8, ln_u[:], ALU.mult, ALU.add)
+        drop = sb.tile([P, U], F32)
+        nc.vector.tensor_tensor(drop[:], win[:].indirect(lo_t[:]), neg_up[:], ALU.add)
+
+        a_t = sb.tile([P, S], F32)
+        b_t = sb.tile([P, S], F32)
+        diff = sb.tile([P, S], F32)
+        root = sb.tile([P, S], F32)
+        nc.scalar.activation(a_t[:], ln_u[:], ACT.Exp, scale=-0.125, bias=math.log(2.0))
+        for h in range(2):
+            nc.scalar.activation(b_t[:, halves[h]], zz[:, halves[h]], ACT.Exp, scale=-0.625, bias=math.log(2.0))
+        for h in range(2):
+            nc.vector.tensor_tensor(diff[:, halves[h]], a_t[:, halves[h]], b_t[:, halves[h]], ALU.subtract)
+            nc.scalar.activation(root[:, halves[h]], diff[:, halves[h]], ACT.Abs)
+
+        part = sb.tile([P, U], F32)
+        res = sb.tile([P, U], F32)
+        for h in range(2):
+            nc.vector.tensor_tensor(part[:, halves[h]], root[:].indirect(up_t[:, list_halves[h]]), drop[:, halves[h]], ALU.mult)
+        for h in range(2):
+            nc.vector.tensor_tensor(res[:, halves[h]], root[:].indirect(lo_t[:, list_halves[h]]), part[:, halves[h]], ALU.mult)
+            nc.sync.dma_start(out[:, halves[h]], res[:, halves[h]])

@@ -18,13 +18,22 @@ ALU = mybir.AluOpType
 ACT = mybir.ActivationFunctionType
 
 P = 128
-HALF = S // 2
+
+
+def cuts(widths):
+    res, a = [], 0
+    for w in widths:
+        res.append(slice(a, a + w))
+        a = a + w
+    return res
+
+
+def cols(sl):
+    return slice(sl.start // 16, sl.stop // 16)
 
 
 def tile_picked_yrich_geo_p_kernel(tc, x_words, x_scales, w1, one, alpha, offs, up, lo, out):
     nc = tc.nc
-    halves = [slice(0, HALF), slice(HALF, S)]
-    list_halves = [slice(0, HALF // 16), slice(HALF // 16, S // 16)]
     with ExitStack() as ctx:
         sb = ctx.enter_context(tc.tile_pool(name="sb", bufs=1))
         ps = ctx.enter_context(tc.psum_pool(name="ps", bufs=1))
@@ -32,8 +41,8 @@ def tile_picked_yrich_geo_p_kernel(tc, x_words, x_scales, w1, one, alpha, offs, 
         offs_t = sb.tile([P, S // 16], U16)
         up_t = sb.tile([P, U // 16], U16)
         lo_t = sb.tile([P, U // 16], U16)
-        words = sb.tile([P, T], U32)
-        scales = sb.tile([P, T], U8)
+        words = sb.tile([P, T], U32, align_bytes=64, tag="slot_a")
+        scales = sb.tile([P, T], U8, align_bytes=64, tag="slot_b")
         w_raw = sb.tile([P, 4, N], F32)
         one_col = sb.tile([P, 4], F32)
         alpha_col = sb.tile([P, 1], F32)
@@ -41,11 +50,12 @@ def tile_picked_yrich_geo_p_kernel(tc, x_words, x_scales, w1, one, alpha, offs, 
         nc.vector.memset(scales[:].bitcast(I32), 0)
         nc.sync.dma_start(offs_t[:], offs)
         for q in range(4):
-            nc.sync.dma_start(scales[32 * q : 32 * q + 4, :].bitcast(I32), x_scales[0, 4 * q : 4 * q + 4, :].bitcast(I32))
+            queue = nc.sync
+            queue.dma_start(scales[32 * q : 32 * q + 4, :].bitcast(I32), x_scales[0, 4 * q : 4 * q + 4, :].bitcast(I32))
         nc.sync.dma_start(words[:].bitcast(I32), x_words[0].rearrange("p n t -> p (n t)").bitcast(I32))
-        nc.gpsimd.dma_start(w_raw[:], w1.rearrange("(p j) n -> p j n", j=4))
-        nc.gpsimd.dma_start(alpha_col[:], alpha)
+        nc.sync.dma_start(w_raw[:], w1.rearrange("(p j) n -> p j n", j=4))
         nc.gpsimd.dma_start(one_col[:], one[0, :].rearrange("(p j) -> p j", j=4))
+        nc.gpsimd.dma_start(alpha_col[:], alpha)
         nc.sync.dma_start(up_t[:], up)
         nc.sync.dma_start(lo_t[:], lo)
 
@@ -58,17 +68,20 @@ def tile_picked_yrich_geo_p_kernel(tc, x_words, x_scales, w1, one, alpha, offs, 
         root_alpha_tenth = sb.tile([P, 1], F32)
         nc.gpsimd.tensor_scalar(root_alpha_tenth[:], root_alpha[:], 0.1, 0.0, ALU.mult, ALU.add)
 
-        w_bf = sb.tile([P, N, 4], BF16, align_bytes=64)
+        w_bf = sb.tile([P, N, 4], BF16, align_bytes=64, tag="staging")
         nc.scalar.copy(w_bf[:], w_raw[:].rearrange("p j n -> p n j"))
         w_codes = sb.tile([P, N], U32, align_bytes=64)
         w_scales = sb.tile([P, N], U8, align_bytes=64)
         x_codes = sb.tile([P, S], U32, align_bytes=64)
-        x_sc = sb.tile([P, S], U8, align_bytes=64)
-        nc.vector.tensor_copy(x_codes[:, halves[0]], words[:].indirect(offs_t[:, list_halves[0]]))
-        nc.vector.tensor_copy(x_sc[:, halves[0]], scales[:].indirect(offs_t[:, list_halves[0]]))
+        head = cuts([256,128,128])
+        for c in head:
+            nc.vector.tensor_copy(x_codes[:, c], words[:].indirect(offs_t[:, cols(c)]))
         nc.vector.quantize_mx(out=w_codes[:].bitcast(FP8X4), scales=w_scales[:], in_=w_bf[:].rearrange("p n j -> p (n j)"))
-        nc.vector.tensor_copy(x_codes[:, halves[1]], words[:].indirect(offs_t[:, list_halves[1]]))
-        nc.vector.tensor_copy(x_sc[:, halves[1]], scales[:].indirect(offs_t[:, list_halves[1]]))
+        x_scs = []
+        for i, c in enumerate(head):
+            x_sc = sb.tile([P, c.stop - c.start], U8, align_bytes=64, name=f"x_sc{i}", tag=["slot_a", "staging", "x_sc2"][i])
+            nc.vector.tensor_copy(x_sc[:], scales[:].indirect(offs_t[:, cols(c)]))
+            x_scs.append(x_sc)
 
         win = sb.tile([P, 4 * S], F32)
         soft = win[:, 0:S]
@@ -77,60 +90,69 @@ def tile_picked_yrich_geo_p_kernel(tc, x_words, x_scales, w1, one, alpha, offs, 
         zz = win[:, 2 * S : 3 * S]
         one_plus = win[:, 3 * S : 4 * S]
 
-        y = [ps.tile([P, HALF], F32, name=f"y{h}") for h in range(2)]
-        for h in range(2):
-            nc.tensor.matmul_mx(out=y[h][:], lhsT=w_codes[:].bitcast(FP8X4), lhsT_scale=w_scales[:],
-                                rhs=x_codes[:, halves[h]].bitcast(FP8X4), rhs_scale=x_sc[:, halves[h]],
+        ys = [ps.tile([P, c.stop - c.start], F32, name=f"y{i}") for i, c in enumerate(head)]
+        for y, c, x_sc in zip(ys, head, x_scs):
+            nc.tensor.matmul_mx(out=y[:], lhsT=w_codes[:].bitcast(FP8X4), lhsT_scale=w_scales[:],
+                                rhs=x_codes[:, c].bitcast(FP8X4), rhs_scale=x_sc[:],
                                 start=True, stop=True)
-            nc.scalar.activation(expy[:, halves[h]], y[h][:], ACT.Exp)
+            nc.scalar.activation(expy[:, c], y[:], ACT.Exp)
         nc.vector.tensor_scalar(one_plus, expy, 2.0**60, 1.0, ALU.min, ALU.add)
 
-        inv_one = sb.tile([P, 4], F32)
-        nc.vector.reciprocal(inv_one[:], one_col[:])
-        inv_one2 = sb.tile([P, 4], F32)
-        nc.vector.tensor_tensor(inv_one2[:], inv_one[:], inv_one[:], ALU.mult)
+        def y_of(c):
+            for y, h in zip(ys, head):
+                if h.start <= c.start and c.stop <= h.stop:
+                    return y[:, c.start - h.start : c.stop - h.start]
+            raise ValueError("chunk")
+
+        inv = sb.tile([P, 8], F32, align_bytes=64, tag="slot_b")
+        nc.vector.reciprocal(inv[:, 0:4], one_col[:])
+        nc.vector.tensor_tensor(inv[:, 4:8], inv[:, 0:4], inv[:, 0:4], ALU.mult)
         k2 = ps.tile([P, 4, P], F32)
         for j in range(4):
-            nc.tensor.transpose(k2[:, j, :], inv_one2[:, j : j + 1].to_broadcast([P, P]), ident[:])
+            nc.tensor.transpose(k2[:, j, :], inv[:, 4 + j : 5 + j].to_broadcast([P, P]), ident[:])
         k2_cells = k2[:].rearrange("p j c -> p c j")
 
         lg = sb.tile([P, S], F32)
         sq = sb.tile([P, S], F32)
         ln_u = sb.tile([P, S], F32)
         ln_v = sb.tile([P, S], F32)
-        for h in range(2):
-            nc.scalar.activation(lg[:, halves[h]], one_plus[:, halves[h]], ACT.Ln)
-            nc.vector.tensor_tensor(soft[:, halves[h]], y[h][:], lg[:, halves[h]], ALU.max)
-        for h in range(2):
-            nc.scalar.activation(sq[:, halves[h]], soft[:, halves[h]], ACT.Square, scale=root_alpha[:], bias=root_alpha_tenth[:])
-            nc.vector.scalar_tensor_tensor(inv_sat2[:, halves[h]].rearrange("p (c j) -> p c j", j=4),
-                                           sq[:, halves[h]].rearrange("p (c j) -> p c j", j=4), 1.0,
-                                           k2_cells[:, 64 * h : 64 * h + 64, :], ALU.add, ALU.mult)
-        for h in range(2):
-            nc.scalar.activation(ln_v[:, halves[h]], inv_sat2[:, halves[h]], ACT.Ln, scale=1.001, bias=-1.0)
-            nc.scalar.activation(ln_u[:, halves[h]], inv_sat2[:, halves[h]], ACT.Ln)
+        mid = cuts([128,128,128,128])
+        for c in mid:
+            nc.scalar.activation(lg[:, c], one_plus[:, c], ACT.Ln)
+            nc.vector.tensor_tensor(soft[:, c], y_of(c), lg[:, c], ALU.max)
+        for c in mid:
+            nc.scalar.activation(sq[:, c], soft[:, c], ACT.Square, scale=root_alpha[:], bias=root_alpha_tenth[:])
+            nc.vector.scalar_tensor_tensor(inv_sat2[:, c].rearrange("p (c j) -> p c j", j=4),
+                                           sq[:, c].rearrange("p (c j) -> p c j", j=4), 1.0,
+                                           k2_cells[:, c.start // 4 : c.stop // 4, :], ALU.add, ALU.mult)
+        for c in mid:
+            nc.scalar.activation(ln_v[:, c], inv_sat2[:, c], ACT.Ln, scale=1.001, bias=-1.0)
+            nc.scalar.activation(ln_u[:, c], inv_sat2[:, c], ACT.Ln)
 
         neg_up = sb.tile([P, U], F32)
         nc.vector.tensor_scalar(neg_up[:], win[:].indirect(up_t[:]), -1.0, 1.0, ALU.mult, ALU.add)
         nc.vector.scalar_tensor_tensor(zz, ln_v[:], -0.8, ln_u[:], ALU.mult, ALU.add)
         drop = sb.tile([P, U], F32)
-        nc.vector.tensor_tensor(drop[:], win[:].indirect(lo_t[:]), neg_up[:], ALU.add)
+        d_cuts = cuts([256,256])
+        nc.vector.tensor_tensor(drop[:, d_cuts[0]], win[:].indirect(lo_t[:, cols(d_cuts[0])]), neg_up[:, d_cuts[0]], ALU.add)
 
         a_t = sb.tile([P, S], F32)
         b_t = sb.tile([P, S], F32)
-        diff = sb.tile([P, S], F32)
+        diff = win[:, 3 * S : 4 * S]
         root = sb.tile([P, S], F32)
+        post = cuts([256,128,128])
         nc.scalar.activation(a_t[:], ln_u[:], ACT.Exp, scale=-0.125, bias=math.log(2.0))
-        for h in range(2):
-            nc.scalar.activation(b_t[:, halves[h]], zz[:, halves[h]], ACT.Exp, scale=-0.625, bias=math.log(2.0))
-        for h in range(2):
-            nc.vector.tensor_tensor(diff[:, halves[h]], a_t[:, halves[h]], b_t[:, halves[h]], ALU.subtract)
-            nc.scalar.activation(root[:, halves[h]], diff[:, halves[h]], ACT.Abs)
+        for c in post:
+            nc.scalar.activation(b_t[:, c], zz[:, c], ACT.Exp, scale=-0.625, bias=math.log(2.0))
+        for c in post:
+            nc.vector.tensor_tensor(diff[:, c], a_t[:, c], b_t[:, c], ALU.subtract)
+            nc.scalar.activation(root[:, c], diff[:, c], ACT.Abs)
+        nc.vector.tensor_tensor(drop[:, d_cuts[1]], win[:].indirect(lo_t[:, cols(d_cuts[1])]), neg_up[:, d_cuts[1]], ALU.add)
 
         part = sb.tile([P, U], F32)
         res = sb.tile([P, U], F32)
-        for h in range(2):
-            nc.vector.tensor_tensor(part[:, halves[h]], root[:].indirect(up_t[:, list_halves[h]]), drop[:, halves[h]], ALU.mult)
-        for h in range(2):
-            nc.vector.tensor_tensor(res[:, halves[h]], root[:].indirect(lo_t[:, list_halves[h]]), part[:, halves[h]], ALU.mult)
-            nc.sync.dma_start(out[:, halves[h]], res[:, halves[h]])
+        for c in cuts([256,256]):
+            nc.vector.tensor_tensor(part[:, c], root[:].indirect(up_t[:, cols(c)]), drop[:, c], ALU.mult)
+        for c in cuts([384,128]):
+            nc.vector.tensor_tensor(res[:, c], root[:].indirect(lo_t[:, cols(c)]), part[:, c], ALU.mult)
+            nc.sync.dma_start(out[:, c], res[:, c])

@@ -47,15 +47,16 @@ def tile_picked_yrich_geo_p_kernel(tc, x_words, x_scales, w1, one, alpha, offs, 
         one_col = sb.tile([P, 4], F32)
         alpha_col = sb.tile([P, 1], F32)
 
-        nc.vector.memset(scales[:].bitcast(I32), 0)
+        nc.vector.memset(scales[:, : T // 2].bitcast(I32), 0)
+        nc.gpsimd.memset(scales[:, T // 2 :].bitcast(I32), 0)
         nc.sync.dma_start(offs_t[:], offs)
         for q in range(4):
             queue = nc.sync
             queue.dma_start(scales[32 * q : 32 * q + 4, :].bitcast(I32), x_scales[0, 4 * q : 4 * q + 4, :].bitcast(I32))
+        nc.scalar.dma_start(w_raw[:], w1.rearrange("(p j) n -> p j n", j=4))
         nc.sync.dma_start(words[:].bitcast(I32), x_words[0].rearrange("p n t -> p (n t)").bitcast(I32))
-        nc.sync.dma_start(w_raw[:], w1.rearrange("(p j) n -> p j n", j=4))
-        nc.gpsimd.dma_start(one_col[:], one[0, :].rearrange("(p j) -> p j", j=4))
-        nc.gpsimd.dma_start(alpha_col[:], alpha)
+        nc.sync.dma_start(one_col[:], one[0, :].rearrange("(p j) -> p j", j=4))
+        nc.sync.dma_start(alpha_col[:], alpha)
         nc.sync.dma_start(up_t[:], up)
         nc.sync.dma_start(lo_t[:], lo)
 
@@ -63,25 +64,19 @@ def tile_picked_yrich_geo_p_kernel(tc, x_words, x_scales, w1, one, alpha, offs, 
         make_identity(nc, ident[:])
         half_t = sb.tile([P, 1], F32)
         nc.gpsimd.memset(half_t[:], 0.5)
-        root_alpha = sb.tile([P, 1], F32)
-        nc.gpsimd.tensor_tensor(root_alpha[:], alpha_col[:], half_t[:], ALU.pow)
-        root_alpha_tenth = sb.tile([P, 1], F32)
-        nc.gpsimd.tensor_scalar(root_alpha_tenth[:], root_alpha[:], 0.1, 0.0, ALU.mult, ALU.add)
 
         w_bf = sb.tile([P, N, 4], BF16, align_bytes=64, tag="staging")
-        nc.scalar.copy(w_bf[:], w_raw[:].rearrange("p j n -> p n j"))
+        nc.vector.tensor_copy(w_bf[:], w_raw[:].rearrange("p j n -> p n j"))
         w_codes = sb.tile([P, N], U32, align_bytes=64)
         w_scales = sb.tile([P, N], U8, align_bytes=64)
-        x_codes = sb.tile([P, S], U32, align_bytes=64)
         head = cuts([256,128,128])
+        nc.vector.quantize_mx(out=w_codes[:].bitcast(FP8X4), scales=w_scales[:], in_=w_bf[:].rearrange("p n j -> p (n j)"))
+        picked_sc = sb.tile([P, S], U8, align_bytes=64)
+        x_scs = [picked_sc[:, c] for c in head]
+        nc.vector.tensor_copy(picked_sc[:], scales[:].indirect(offs_t[:]))
+        x_codes = sb.tile([P, S], U32, align_bytes=64, tag="slot_b")
         for c in head:
             nc.vector.tensor_copy(x_codes[:, c], words[:].indirect(offs_t[:, cols(c)]))
-        nc.vector.quantize_mx(out=w_codes[:].bitcast(FP8X4), scales=w_scales[:], in_=w_bf[:].rearrange("p n j -> p (n j)"))
-        x_scs = []
-        for i, c in enumerate(head):
-            x_sc = sb.tile([P, c.stop - c.start], U8, align_bytes=64, name=f"x_sc{i}", tag=["slot_a", "staging", "x_sc2"][i])
-            nc.vector.tensor_copy(x_sc[:], scales[:].indirect(offs_t[:, cols(c)]))
-            x_scs.append(x_sc)
 
         win = sb.tile([P, 4 * S], F32)
         soft = win[:, 0:S]
@@ -93,7 +88,7 @@ def tile_picked_yrich_geo_p_kernel(tc, x_words, x_scales, w1, one, alpha, offs, 
         ys = [ps.tile([P, c.stop - c.start], F32, name=f"y{i}") for i, c in enumerate(head)]
         for y, c, x_sc in zip(ys, head, x_scs):
             nc.tensor.matmul_mx(out=y[:], lhsT=w_codes[:].bitcast(FP8X4), lhsT_scale=w_scales[:],
-                                rhs=x_codes[:, c].bitcast(FP8X4), rhs_scale=x_sc[:],
+                                rhs=x_codes[:, c].bitcast(FP8X4), rhs_scale=x_sc,
                                 start=True, stop=True)
             nc.scalar.activation(expy[:, c], y[:], ACT.Exp)
         nc.vector.tensor_scalar(one_plus, expy, 2.0**60, 1.0, ALU.min, ALU.add)
@@ -104,7 +99,11 @@ def tile_picked_yrich_geo_p_kernel(tc, x_words, x_scales, w1, one, alpha, offs, 
                     return y[:, c.start - h.start : c.stop - h.start]
             raise ValueError("chunk")
 
-        inv = sb.tile([P, 8], F32, align_bytes=64, tag="slot_b")
+        inv = sb.tile([P, 16], F32, align_bytes=64, tag="slot_a")
+        root_alpha = inv[:, 8:9]
+        root_alpha_tenth = inv[:, 9:10]
+        nc.gpsimd.tensor_tensor(root_alpha, alpha_col[:], half_t[:], ALU.pow)
+        nc.gpsimd.tensor_scalar(root_alpha_tenth, root_alpha, 0.1, 0.0, ALU.mult, ALU.add)
         nc.vector.reciprocal(inv[:, 0:4], one_col[:])
         nc.vector.tensor_tensor(inv[:, 4:8], inv[:, 0:4], inv[:, 0:4], ALU.mult)
         k2 = ps.tile([P, 4, P], F32)
@@ -121,11 +120,11 @@ def tile_picked_yrich_geo_p_kernel(tc, x_words, x_scales, w1, one, alpha, offs, 
             nc.scalar.activation(lg[:, c], one_plus[:, c], ACT.Ln)
             nc.vector.tensor_tensor(soft[:, c], y_of(c), lg[:, c], ALU.max)
         for c in mid:
-            nc.scalar.activation(sq[:, c], soft[:, c], ACT.Square, scale=root_alpha[:], bias=root_alpha_tenth[:])
+            nc.scalar.activation(sq[:, c], soft[:, c], ACT.Square, scale=root_alpha, bias=root_alpha_tenth)
             nc.vector.scalar_tensor_tensor(inv_sat2[:, c].rearrange("p (c j) -> p c j", j=4),
                                            sq[:, c].rearrange("p (c j) -> p c j", j=4), 1.0,
                                            k2_cells[:, c.start // 4 : c.stop // 4, :], ALU.add, ALU.mult)
-        for c in mid:
+        for c in cuts([128,128,256]):
             nc.scalar.activation(ln_v[:, c], inv_sat2[:, c], ACT.Ln, scale=1.001, bias=-1.0)
             nc.scalar.activation(ln_u[:, c], inv_sat2[:, c], ACT.Ln)
 
@@ -133,14 +132,14 @@ def tile_picked_yrich_geo_p_kernel(tc, x_words, x_scales, w1, one, alpha, offs, 
         nc.vector.tensor_scalar(neg_up[:], win[:].indirect(up_t[:]), -1.0, 1.0, ALU.mult, ALU.add)
         nc.vector.scalar_tensor_tensor(zz, ln_v[:], -0.8, ln_u[:], ALU.mult, ALU.add)
         drop = sb.tile([P, U], F32)
-        d_cuts = cuts([256,256])
+        d_cuts = cuts([384,128])
         nc.vector.tensor_tensor(drop[:, d_cuts[0]], win[:].indirect(lo_t[:, cols(d_cuts[0])]), neg_up[:, d_cuts[0]], ALU.add)
 
         a_t = sb.tile([P, S], F32)
         b_t = sb.tile([P, S], F32)
         diff = win[:, 3 * S : 4 * S]
         root = sb.tile([P, S], F32)
-        post = cuts([256,128,128])
+        post = cuts([192,192,128])
         nc.scalar.activation(a_t[:], ln_u[:], ACT.Exp, scale=-0.125, bias=math.log(2.0))
         for c in post:
             nc.scalar.activation(b_t[:, c], zz[:, c], ACT.Exp, scale=-0.625, bias=math.log(2.0))

@@ -18,140 +18,157 @@ ALU = mybir.AluOpType
 ACT = mybir.ActivationFunctionType
 
 P = 128
+PACK = 4
+LIST_ROWS = 16
+EXP_CAP = 2.0**60
+
+HALF, QUARTER = S // 2, S // 4
+HALVES = [HALF, HALF]
+QUARTERS = [QUARTER] * 4
+SHORT_END = [HALF, QUARTER, QUARTER]
+SHORT_START = [QUARTER, QUARTER, HALF]
 
 
-def cuts(widths):
-    res, a = [], 0
-    for w in widths:
-        res.append(slice(a, a + w))
-        a = a + w
-    return res
+def pieces(widths):
+    starts = [sum(widths[:i]) for i in range(len(widths))]
+    return [slice(start, start + width) for start, width in zip(starts, widths)]
 
 
-def cols(sl):
-    return slice(sl.start // 16, sl.stop // 16)
+def list_columns(piece):
+    return slice(piece.start // LIST_ROWS, piece.stop // LIST_ROWS)
 
 
 def tile_picked_yrich_geo_p_kernel(tc, x_words, x_scales, w1, one, alpha, offs, up, lo, out):
     nc = tc.nc
     with ExitStack() as ctx:
         sb = ctx.enter_context(tc.tile_pool(name="sb", bufs=1))
+        shared = ctx.enter_context(tc.tile_pool(name="shared", bufs=1))
         ps = ctx.enter_context(tc.psum_pool(name="ps", bufs=1))
 
-        offs_t = sb.tile([P, S // 16], U16)
-        up_t = sb.tile([P, U // 16], U16)
-        lo_t = sb.tile([P, U // 16], U16)
-        words = sb.tile([P, T], U32, align_bytes=64, tag="slot_a")
-        scales = sb.tile([P, T], U8, align_bytes=64, tag="slot_b")
-        w_raw = sb.tile([P, 4, N], F32)
-        one_col = sb.tile([P, 4], F32)
+        offs_list = sb.tile([P, S // LIST_ROWS], U16)
+        up_list = sb.tile([P, U // LIST_ROWS], U16)
+        lo_list = sb.tile([P, U // LIST_ROWS], U16)
+        words = sb.tile([P, T], U32, align_bytes=64, tag="words_then_constants")
+        scales = shared.tile([P, T], U8, align_bytes=64, offset=0)
+        w_raw = sb.tile([P, PACK, N], F32)
+        one_cols = sb.tile([P, PACK], F32)
         alpha_col = sb.tile([P, 1], F32)
 
         nc.vector.memset(scales[:, : T // 2].bitcast(I32), 0)
         nc.gpsimd.memset(scales[:, T // 2 :].bitcast(I32), 0)
-        nc.sync.dma_start(offs_t[:], offs)
-        for q in range(4):
-            queue = nc.sync
+        nc.sync.dma_start(offs_list[:], offs)
+        nc.scalar.dma_start(w_raw[:], w1.rearrange("(p j) n -> p j n", j=PACK))
+        for q, queue in enumerate([nc.sync, nc.sync, nc.scalar, nc.scalar]):
             queue.dma_start(scales[32 * q : 32 * q + 4, :].bitcast(I32), x_scales[0, 4 * q : 4 * q + 4, :].bitcast(I32))
-        nc.scalar.dma_start(w_raw[:], w1.rearrange("(p j) n -> p j n", j=4))
         nc.sync.dma_start(words[:].bitcast(I32), x_words[0].rearrange("p n t -> p (n t)").bitcast(I32))
-        nc.sync.dma_start(one_col[:], one[0, :].rearrange("(p j) -> p j", j=4))
+        nc.sync.dma_start(one_cols[:], one[0, :].rearrange("(p j) -> p j", j=PACK))
         nc.sync.dma_start(alpha_col[:], alpha)
-        nc.sync.dma_start(up_t[:], up)
-        nc.sync.dma_start(lo_t[:], lo)
+        nc.sync.dma_start(up_list[:], up)
+        nc.sync.dma_start(lo_list[:], lo)
 
-        ident = sb.tile([P, P], F32)
-        make_identity(nc, ident[:])
-        half_t = sb.tile([P, 1], F32)
-        nc.gpsimd.memset(half_t[:], 0.5)
+        identity = sb.tile([P, P], F32)
+        make_identity(nc, identity[:])
+        one_half = sb.tile([P, 1], F32)
+        nc.gpsimd.memset(one_half[:], 0.5)
 
-        w_bf = sb.tile([P, N, 4], BF16, align_bytes=64, tag="staging")
-        nc.vector.tensor_copy(w_bf[:], w_raw[:].rearrange("p j n -> p n j"))
-        w_codes = sb.tile([P, N], U32, align_bytes=64)
+        w_rounded = sb.tile([P, N, PACK], BF16, align_bytes=64)
+        nc.scalar.copy(w_rounded[:], w_raw[:].rearrange("p j n -> p n j"))
+        w_codes = shared.tile([P, N], U32, align_bytes=64, offset=0)
         w_scales = sb.tile([P, N], U8, align_bytes=64)
-        head = cuts([256,128,128])
-        nc.vector.quantize_mx(out=w_codes[:].bitcast(FP8X4), scales=w_scales[:], in_=w_bf[:].rearrange("p n j -> p (n j)"))
-        picked_sc = sb.tile([P, S], U8, align_bytes=64)
-        x_scs = [picked_sc[:, c] for c in head]
-        nc.vector.tensor_copy(picked_sc[:], scales[:].indirect(offs_t[:]))
-        x_codes = sb.tile([P, S], U32, align_bytes=64, tag="slot_b")
-        for c in head:
-            nc.vector.tensor_copy(x_codes[:, c], words[:].indirect(offs_t[:, cols(c)]))
+        x_picked_scales = sb.tile([P, S], U8, align_bytes=64)
+        nc.vector.tensor_copy(x_picked_scales[:], scales[:].indirect(offs_list[:]))
+        nc.vector.quantize_mx(
+            out=w_codes[:].bitcast(FP8X4), scales=w_scales[:], in_=w_rounded[:].rearrange("p n j -> p (n j)")
+        )
+        x_codes = shared.tile([P, S], U32, align_bytes=64, offset=PACK * N)
+        product_pieces = pieces(SHORT_END)
+        for piece in product_pieces:
+            nc.vector.tensor_copy(x_codes[:, piece], words[:].indirect(offs_list[:, list_columns(piece)]))
 
-        win = sb.tile([P, 4 * S], F32)
-        soft = win[:, 0:S]
-        inv_sat2 = win[:, S : 2 * S]
-        expy = win[:, 2 * S : 3 * S]
-        zz = win[:, 2 * S : 3 * S]
-        one_plus = win[:, 3 * S : 4 * S]
+        window = sb.tile([P, 4 * S], F32)
+        soft = window[:, 0:S]
+        inv_sat2 = window[:, S : 2 * S]
+        exp_y = window[:, 2 * S : 3 * S]
+        log_ratio = window[:, 2 * S : 3 * S]
+        one_plus_exp = window[:, 3 * S : 4 * S]
 
-        ys = [ps.tile([P, c.stop - c.start], F32, name=f"y{i}") for i, c in enumerate(head)]
-        for y, c, x_sc in zip(ys, head, x_scs):
-            nc.tensor.matmul_mx(out=y[:], lhsT=w_codes[:].bitcast(FP8X4), lhsT_scale=w_scales[:],
-                                rhs=x_codes[:, c].bitcast(FP8X4), rhs_scale=x_sc,
-                                start=True, stop=True)
-            nc.scalar.activation(expy[:, c], y[:], ACT.Exp)
-        nc.vector.tensor_scalar(one_plus, expy, 2.0**60, 1.0, ALU.min, ALU.add)
+        banks = [ps.tile([P, width], F32, name=f"y{i}") for i, width in enumerate(SHORT_END)]
+        for bank, piece in zip(banks, product_pieces):
+            nc.tensor.matmul_mx(
+                out=bank[:],
+                lhsT=w_codes[:].bitcast(FP8X4),
+                lhsT_scale=w_scales[:],
+                rhs=x_codes[:, piece].bitcast(FP8X4),
+                rhs_scale=x_picked_scales[:, piece],
+                start=True,
+                stop=True,
+            )
+            nc.scalar.activation(exp_y[:, piece], bank[:], ACT.Exp)
+        nc.vector.tensor_scalar(one_plus_exp, exp_y, EXP_CAP, 1.0, ALU.min, ALU.add)
+        y_quarters = [banks[0][:, :QUARTER], banks[0][:, QUARTER:], banks[1][:], banks[2][:]]
 
-        def y_of(c):
-            for y, h in zip(ys, head):
-                if h.start <= c.start and c.stop <= h.stop:
-                    return y[:, c.start - h.start : c.stop - h.start]
-            raise ValueError("chunk")
+        constants = sb.tile([P, 16], F32, align_bytes=64, tag="words_then_constants")
+        inv_one = constants[:, 0:PACK]
+        inv_one2 = constants[:, PACK : 2 * PACK]
+        root_alpha = constants[:, 8:9]
+        tenth_root_alpha = constants[:, 9:10]
+        nc.gpsimd.tensor_tensor(root_alpha, alpha_col[:], one_half[:], ALU.pow)
+        nc.gpsimd.tensor_scalar(tenth_root_alpha, root_alpha, 0.1, 0.0, ALU.mult, ALU.add)
+        nc.vector.reciprocal(inv_one, one_cols[:])
+        nc.vector.tensor_tensor(inv_one2, inv_one, inv_one, ALU.mult)
+        inv_one2_rows = ps.tile([P, PACK, P], F32)
+        for j in range(PACK):
+            nc.tensor.transpose(inv_one2_rows[:, j, :], inv_one2[:, j : j + 1].to_broadcast([P, P]), identity[:])
+        inv_one2_cells = inv_one2_rows[:].rearrange("p j c -> p c j")
 
-        inv = sb.tile([P, 16], F32, align_bytes=64, tag="slot_a")
-        root_alpha = inv[:, 8:9]
-        root_alpha_tenth = inv[:, 9:10]
-        nc.gpsimd.tensor_tensor(root_alpha, alpha_col[:], half_t[:], ALU.pow)
-        nc.gpsimd.tensor_scalar(root_alpha_tenth, root_alpha, 0.1, 0.0, ALU.mult, ALU.add)
-        nc.vector.reciprocal(inv[:, 0:4], one_col[:])
-        nc.vector.tensor_tensor(inv[:, 4:8], inv[:, 0:4], inv[:, 0:4], ALU.mult)
-        k2 = ps.tile([P, 4, P], F32)
-        for j in range(4):
-            nc.tensor.transpose(k2[:, j, :], inv[:, 4 + j : 5 + j].to_broadcast([P, P]), ident[:])
-        k2_cells = k2[:].rearrange("p j c -> p c j")
+        log_one_plus_exp = sb.tile([P, S], F32)
+        alpha_suc2 = sb.tile([P, S], F32)
+        log_inv_sat2 = sb.tile([P, S], F32)
+        log_numerator = sb.tile([P, S], F32)
+        for piece, y in zip(pieces(QUARTERS), y_quarters):
+            nc.scalar.activation(log_one_plus_exp[:, piece], one_plus_exp[:, piece], ACT.Ln)
+            nc.vector.tensor_tensor(soft[:, piece], y, log_one_plus_exp[:, piece], ALU.max)
+        for piece in pieces(QUARTERS):
+            nc.scalar.activation(
+                alpha_suc2[:, piece], soft[:, piece], ACT.Square, scale=root_alpha, bias=tenth_root_alpha
+            )
+            nc.vector.scalar_tensor_tensor(
+                inv_sat2[:, piece].rearrange("p (c j) -> p c j", j=PACK),
+                alpha_suc2[:, piece].rearrange("p (c j) -> p c j", j=PACK),
+                1.0,
+                inv_one2_cells[:, piece.start // PACK : piece.stop // PACK, :],
+                ALU.add,
+                ALU.mult,
+            )
+        for piece in pieces(SHORT_START):
+            nc.scalar.activation(log_numerator[:, piece], inv_sat2[:, piece], ACT.Ln, scale=1.001, bias=-1.0)
+            nc.scalar.activation(log_inv_sat2[:, piece], inv_sat2[:, piece], ACT.Ln)
 
-        lg = sb.tile([P, S], F32)
-        sq = sb.tile([P, S], F32)
-        ln_u = sb.tile([P, S], F32)
-        ln_v = sb.tile([P, S], F32)
-        mid = cuts([128,128,128,128])
-        for c in mid:
-            nc.scalar.activation(lg[:, c], one_plus[:, c], ACT.Ln)
-            nc.vector.tensor_tensor(soft[:, c], y_of(c), lg[:, c], ALU.max)
-        for c in mid:
-            nc.scalar.activation(sq[:, c], soft[:, c], ACT.Square, scale=root_alpha, bias=root_alpha_tenth)
-            nc.vector.scalar_tensor_tensor(inv_sat2[:, c].rearrange("p (c j) -> p c j", j=4),
-                                           sq[:, c].rearrange("p (c j) -> p c j", j=4), 1.0,
-                                           k2_cells[:, c.start // 4 : c.stop // 4, :], ALU.add, ALU.mult)
-        for c in cuts([128,128,256]):
-            nc.scalar.activation(ln_v[:, c], inv_sat2[:, c], ACT.Ln, scale=1.001, bias=-1.0)
-            nc.scalar.activation(ln_u[:, c], inv_sat2[:, c], ACT.Ln)
+        one_minus_up = sb.tile([P, U], F32)
+        nc.vector.tensor_scalar(one_minus_up[:], window[:].indirect(up_list[:]), -1.0, 1.0, ALU.mult, ALU.add)
+        nc.vector.tensor_tensor(log_ratio, log_numerator[:], log_inv_sat2[:], ALU.subtract)
+        drive = sb.tile([P, U], F32)
+        nc.vector.tensor_tensor(drive[:], window[:].indirect(lo_list[:]), one_minus_up[:], ALU.add)
 
-        neg_up = sb.tile([P, U], F32)
-        nc.vector.tensor_scalar(neg_up[:], win[:].indirect(up_t[:]), -1.0, 1.0, ALU.mult, ALU.add)
-        nc.vector.scalar_tensor_tensor(zz, ln_v[:], -0.8, ln_u[:], ALU.mult, ALU.add)
-        drop = sb.tile([P, U], F32)
-        d_cuts = cuts([384,128])
-        nc.vector.tensor_tensor(drop[:, d_cuts[0]], win[:].indirect(lo_t[:, cols(d_cuts[0])]), neg_up[:, d_cuts[0]], ALU.add)
-
-        a_t = sb.tile([P, S], F32)
-        b_t = sb.tile([P, S], F32)
-        diff = win[:, 3 * S : 4 * S]
+        two_sat_quarter_power = sb.tile([P, S], F32)
+        sqrt_term = sb.tile([P, S], F32)
+        abs_term = sb.tile([P, S], F32)
         root = sb.tile([P, S], F32)
-        post = cuts([192,192,128])
-        nc.scalar.activation(a_t[:], ln_u[:], ACT.Exp, scale=-0.125, bias=math.log(2.0))
-        for c in post:
-            nc.scalar.activation(b_t[:, c], zz[:, c], ACT.Exp, scale=-0.625, bias=math.log(2.0))
-        for c in post:
-            nc.vector.tensor_tensor(diff[:, c], a_t[:, c], b_t[:, c], ALU.subtract)
-            nc.scalar.activation(root[:, c], diff[:, c], ACT.Abs)
-        nc.vector.tensor_tensor(drop[:, d_cuts[1]], win[:].indirect(lo_t[:, cols(d_cuts[1])]), neg_up[:, d_cuts[1]], ALU.add)
+        nc.scalar.activation(two_sat_quarter_power[:], log_inv_sat2[:], ACT.Exp, scale=-0.125, bias=math.log(2.0))
+        for piece in pieces(HALVES):
+            nc.scalar.activation(sqrt_term[:, piece], log_ratio[:, piece], ACT.Exp, scale=0.5)
+        for piece in pieces(SHORT_END):
+            nc.scalar.activation(abs_term[:, piece], sqrt_term[:, piece], ACT.Abs, scale=-1.0, bias=1.0)
+            nc.vector.tensor_tensor(root[:, piece], abs_term[:, piece], two_sat_quarter_power[:, piece], ALU.mult)
 
-        part = sb.tile([P, U], F32)
-        res = sb.tile([P, U], F32)
-        for c in cuts([256,256]):
-            nc.vector.tensor_tensor(part[:, c], root[:].indirect(up_t[:, cols(c)]), drop[:, c], ALU.mult)
-        for c in cuts([384,128]):
-            nc.vector.tensor_tensor(res[:, c], root[:].indirect(lo_t[:, cols(c)]), part[:, c], ALU.mult)
-            nc.sync.dma_start(out[:, c], res[:, c])
+        up_drive = sb.tile([P, U], F32)
+        flux = sb.tile([P, U], F32)
+        for piece in pieces(HALVES):
+            nc.vector.tensor_tensor(
+                up_drive[:, piece], root[:].indirect(up_list[:, list_columns(piece)]), drive[:, piece], ALU.mult
+            )
+        for piece in pieces(SHORT_END):
+            nc.vector.tensor_tensor(
+                flux[:, piece], root[:].indirect(lo_list[:, list_columns(piece)]), up_drive[:, piece], ALU.mult
+            )
+            nc.sync.dma_start(out[:, piece], flux[:, piece])

@@ -42,14 +42,13 @@ def tile_picked_yrich_geo_p_kernel(tc, x_words, x_scales, w1, one, alpha, offs, 
     nc = tc.nc
     with ExitStack() as ctx:
         sb = ctx.enter_context(tc.tile_pool(name="sb", bufs=1))
-        shared = ctx.enter_context(tc.tile_pool(name="shared", bufs=1))
         ps = ctx.enter_context(tc.psum_pool(name="ps", bufs=1))
 
         offs_list = sb.tile([P, S // LIST_ROWS], U16)
         up_list = sb.tile([P, U // LIST_ROWS], U16)
         lo_list = sb.tile([P, U // LIST_ROWS], U16)
         words = sb.tile([P, T], U32, align_bytes=64, tag="words_then_constants")
-        scales = shared.tile([P, T], U8, align_bytes=64, offset=0)
+        scales = sb.tile([P, T], U8, align_bytes=64)
         w_raw = sb.tile([P, PACK, N], F32)
         one_cols = sb.tile([P, PACK], F32)
         alpha_col = sb.tile([P, 1], F32)
@@ -73,23 +72,22 @@ def tile_picked_yrich_geo_p_kernel(tc, x_words, x_scales, w1, one, alpha, offs, 
 
         w_rounded = sb.tile([P, N, PACK], BF16, align_bytes=64)
         nc.scalar.copy(w_rounded[:], w_raw[:].rearrange("p j n -> p n j"))
-        w_codes = shared.tile([P, N], U32, align_bytes=64, offset=0)
+        w_codes = sb.tile([P, N], U32, align_bytes=64)
         w_scales = sb.tile([P, N], U8, align_bytes=64)
         x_picked_scales = sb.tile([P, S], U8, align_bytes=64)
         nc.vector.tensor_copy(x_picked_scales[:], scales[:].indirect(offs_list[:]))
         nc.vector.quantize_mx(
             out=w_codes[:].bitcast(FP8X4), scales=w_scales[:], in_=w_rounded[:].rearrange("p n j -> p (n j)")
         )
-        x_codes = shared.tile([P, S], U32, align_bytes=64, offset=PACK * N)
+        x_codes = sb.tile([P, S], U32, align_bytes=64)
         product_pieces = pieces(SHORT_END)
         for piece in product_pieces:
             nc.vector.tensor_copy(x_codes[:, piece], words[:].indirect(offs_list[:, list_columns(piece)]))
 
         window = sb.tile([P, 4 * S], F32)
         soft = window[:, 0:S]
-        inv_sat2 = window[:, S : 2 * S]
+        alpha_suc2 = window[:, S : 2 * S]
         exp_y = window[:, 2 * S : 3 * S]
-        log_ratio = window[:, 2 * S : 3 * S]
         one_plus_exp = window[:, 3 * S : 4 * S]
 
         banks = [ps.tile([P, width], F32, name=f"y{i}") for i, width in enumerate(SHORT_END)]
@@ -122,7 +120,7 @@ def tile_picked_yrich_geo_p_kernel(tc, x_words, x_scales, w1, one, alpha, offs, 
         inv_one2_cells = inv_one2_rows[:].rearrange("p j c -> p c j")
 
         log_one_plus_exp = sb.tile([P, S], F32)
-        alpha_suc2 = sb.tile([P, S], F32)
+        inv_sat2 = sb.tile([P, S], F32)
         log_inv_sat2 = sb.tile([P, S], F32)
         log_numerator = sb.tile([P, S], F32)
         for piece, y in zip(pieces(QUARTERS), y_quarters):
@@ -146,20 +144,28 @@ def tile_picked_yrich_geo_p_kernel(tc, x_words, x_scales, w1, one, alpha, offs, 
 
         one_minus_up = sb.tile([P, U], F32)
         nc.vector.tensor_scalar(one_minus_up[:], window[:].indirect(up_list[:]), -1.0, 1.0, ALU.mult, ALU.add)
-        nc.vector.tensor_tensor(log_ratio, log_numerator[:], log_inv_sat2[:], ALU.subtract)
-        drive = sb.tile([P, U], F32)
+        first, second = pieces(HALVES)
+        half_sign = sb.tile([P, HALF], F32)
+        nc.vector.tensor_scalar(half_sign[:], inv_sat2[:, second], 1000.0, 0.5, ALU.is_gt, ALU.subtract)
+        log_ratio = sb.tile([P, S], F32)
+        nc.vector.tensor_tensor(log_ratio[:], log_numerator[:], log_inv_sat2[:], ALU.subtract)
+        drive = inv_sat2
         nc.vector.tensor_tensor(drive[:], window[:].indirect(lo_list[:]), one_minus_up[:], ALU.add)
 
-        two_sat_quarter_power = sb.tile([P, S], F32)
+        power = sb.tile([P, S], F32)
         sqrt_term = sb.tile([P, S], F32)
-        abs_term = sb.tile([P, S], F32)
+        half_abs = sb.tile([P, HALF], F32)
+        signed_power = sb.tile([P, HALF], F32)
         root = sb.tile([P, S], F32)
-        nc.scalar.activation(two_sat_quarter_power[:], log_inv_sat2[:], ACT.Exp, scale=-0.125, bias=math.log(2.0))
-        for piece in pieces(HALVES):
+        nc.scalar.activation(power[:], log_inv_sat2[:], ACT.Exp, scale=-0.125, bias=math.log(4.0))
+        for piece in (first, second):
             nc.scalar.activation(sqrt_term[:, piece], log_ratio[:, piece], ACT.Exp, scale=0.5)
-        for piece in pieces(SHORT_END):
-            nc.scalar.activation(abs_term[:, piece], sqrt_term[:, piece], ACT.Abs, scale=-1.0, bias=1.0)
-            nc.vector.tensor_tensor(root[:, piece], abs_term[:, piece], two_sat_quarter_power[:, piece], ALU.mult)
+        nc.scalar.activation(half_abs[:], sqrt_term[:, first], ACT.Abs, scale=-0.5, bias=0.5)
+        nc.vector.tensor_tensor(signed_power[:], half_sign[:], power[:, second], ALU.mult)
+        nc.vector.scalar_tensor_tensor(
+            root[:, second], sqrt_term[:, second], 1.0, signed_power[:], ALU.subtract, ALU.mult
+        )
+        nc.vector.tensor_tensor(root[:, first], half_abs[:], power[:, first], ALU.mult)
 
         up_drive = sb.tile([P, U], F32)
         flux = sb.tile([P, U], F32)

import math
from contextlib import ExitStack

import concourse.mybir as mybir
from concourse.masks import make_identity

K, T, S, N, U = 512, 1024, 512, 128, 512
FLOPS = 2 * K * S * N

F32 = mybir.dt.float32
BF16 = mybir.dt.bfloat16
I32 = mybir.dt.int32
U32 = mybir.dt.uint32
U16 = mybir.dt.uint16
U8 = mybir.dt.uint8
FP8X4 = mybir.dt.float8_e4m3fn_x4
ALU = mybir.AluOpType
ACT = mybir.ActivationFunctionType

P = 128
PACK = 4
LIST_ROWS = 16
EXP_CAP = 2.0**60

HALF, QUARTER = S // 2, S // 4
HALVES = [HALF, HALF]
QUARTERS = [QUARTER] * 4
SHORT_END = [HALF, QUARTER, QUARTER]
SHORT_START = [QUARTER, QUARTER, HALF]


def pieces(widths):
    starts = [sum(widths[:i]) for i in range(len(widths))]
    return [slice(start, start + width) for start, width in zip(starts, widths)]


def list_columns(piece):
    return slice(piece.start // LIST_ROWS, piece.stop // LIST_ROWS)


def tile_picked_yrich_geo_p_kernel(tc, x_words, x_scales, w1, one, alpha, offs, up, lo, out):
    nc = tc.nc
    with ExitStack() as ctx:
        sb = ctx.enter_context(tc.tile_pool(name="sb", bufs=1))
        ps = ctx.enter_context(tc.psum_pool(name="ps", bufs=1))

        offs_list = sb.tile([P, S // LIST_ROWS], U16)
        up_list = sb.tile([P, U // LIST_ROWS], U16)
        lo_list = sb.tile([P, U // LIST_ROWS], U16)
        words = sb.tile([P, T], U32, align_bytes=64, tag="words_then_constants")
        scales = sb.tile([P, T], U8, align_bytes=64)
        w_raw = sb.tile([P, PACK, N], F32)
        one_cols = sb.tile([P, PACK], F32)
        alpha_col = sb.tile([P, 1], F32)

        nc.vector.memset(scales[:, : T // 2].bitcast(I32), 0)
        nc.gpsimd.memset(scales[:, T // 2 :].bitcast(I32), 0)
        nc.sync.dma_start(offs_list[:], offs)
        nc.scalar.dma_start(w_raw[:], w1.rearrange("(p j) n -> p j n", j=PACK))
        for q, queue in enumerate([nc.sync, nc.sync, nc.scalar, nc.scalar]):
            queue.dma_start(scales[32 * q : 32 * q + 4, :].bitcast(I32), x_scales[0, 4 * q : 4 * q + 4, :].bitcast(I32))
        nc.sync.dma_start(words[:].bitcast(I32), x_words[0].rearrange("p n t -> p (n t)").bitcast(I32))
        nc.sync.dma_start(one_cols[:], one[0, :].rearrange("(p j) -> p j", j=PACK))
        nc.sync.dma_start(alpha_col[:], alpha)
        nc.sync.dma_start(up_list[:], up)
        nc.sync.dma_start(lo_list[:], lo)

        identity = sb.tile([P, P], F32)
        make_identity(nc, identity[:])
        one_half = sb.tile([P, 1], F32)
        nc.gpsimd.memset(one_half[:], 0.5)

        w_rounded = sb.tile([P, N, PACK], BF16, align_bytes=64)
        nc.scalar.copy(w_rounded[:], w_raw[:].rearrange("p j n -> p n j"))
        w_codes = sb.tile([P, N], U32, align_bytes=64)
        w_scales = sb.tile([P, N], U8, align_bytes=64)
        x_picked_scales = sb.tile([P, S], U8, align_bytes=64)
        nc.vector.tensor_copy(x_picked_scales[:], scales[:].indirect(offs_list[:]))
        nc.vector.quantize_mx(
            out=w_codes[:].bitcast(FP8X4), scales=w_scales[:], in_=w_rounded[:].rearrange("p n j -> p (n j)")
        )
        x_codes = sb.tile([P, S], U32, align_bytes=64)
        product_pieces = pieces(SHORT_END)
        for piece in product_pieces:
            nc.vector.tensor_copy(x_codes[:, piece], words[:].indirect(offs_list[:, list_columns(piece)]))

        window = sb.tile([P, 4 * S], F32)
        soft = window[:, 0:S]
        alpha_suc2 = window[:, S : 2 * S]
        exp_y = window[:, 2 * S : 3 * S]
        one_plus_exp = window[:, 3 * S : 4 * S]

        banks = [ps.tile([P, width], F32, name=f"y{i}") for i, width in enumerate(SHORT_END)]
        for bank, piece in zip(banks, product_pieces):
            nc.tensor.matmul_mx(
                out=bank[:],
                lhsT=w_codes[:].bitcast(FP8X4),
                lhsT_scale=w_scales[:],
                rhs=x_codes[:, piece].bitcast(FP8X4),
                rhs_scale=x_picked_scales[:, piece],
                start=True,
                stop=True,
            )
            nc.scalar.activation(exp_y[:, piece], bank[:], ACT.Exp)
        nc.vector.tensor_scalar(one_plus_exp, exp_y, EXP_CAP, 1.0, ALU.min, ALU.add)
        y_quarters = [banks[0][:, :QUARTER], banks[0][:, QUARTER:], banks[1][:], banks[2][:]]

        constants = sb.tile([P, 16], F32, align_bytes=64, tag="words_then_constants")
        inv_one = constants[:, 0:PACK]
        inv_one2 = constants[:, PACK : 2 * PACK]
        root_alpha = constants[:, 8:9]
        tenth_root_alpha = constants[:, 9:10]
        nc.gpsimd.tensor_tensor(root_alpha, alpha_col[:], one_half[:], ALU.pow)
        nc.gpsimd.tensor_scalar(tenth_root_alpha, root_alpha, 0.1, 0.0, ALU.mult, ALU.add)
        nc.vector.reciprocal(inv_one, one_cols[:])
        nc.vector.tensor_tensor(inv_one2, inv_one, inv_one, ALU.mult)
        inv_one2_rows = ps.tile([P, PACK, P], F32)
        for j in range(PACK):
            nc.tensor.transpose(inv_one2_rows[:, j, :], inv_one2[:, j : j + 1].to_broadcast([P, P]), identity[:])
        inv_one2_cells = inv_one2_rows[:].rearrange("p j c -> p c j")

        log_one_plus_exp = sb.tile([P, S], F32)
        inv_sat2 = sb.tile([P, S], F32)
        log_inv_sat2 = sb.tile([P, S], F32)
        log_numerator = sb.tile([P, S], F32)
        for piece, y in zip(pieces(QUARTERS), y_quarters):
            nc.scalar.activation(log_one_plus_exp[:, piece], one_plus_exp[:, piece], ACT.Ln)
            nc.vector.tensor_tensor(soft[:, piece], y, log_one_plus_exp[:, piece], ALU.max)
        for piece in pieces(QUARTERS):
            nc.scalar.activation(
                alpha_suc2[:, piece], soft[:, piece], ACT.Square, scale=root_alpha, bias=tenth_root_alpha
            )
            nc.vector.scalar_tensor_tensor(
                inv_sat2[:, piece].rearrange("p (c j) -> p c j", j=PACK),
                alpha_suc2[:, piece].rearrange("p (c j) -> p c j", j=PACK),
                1.0,
                inv_one2_cells[:, piece.start // PACK : piece.stop // PACK, :],
                ALU.add,
                ALU.mult,
            )
        for piece in pieces(SHORT_START):
            nc.scalar.activation(log_numerator[:, piece], inv_sat2[:, piece], ACT.Ln, scale=1.001, bias=-1.0)
            nc.scalar.activation(log_inv_sat2[:, piece], inv_sat2[:, piece], ACT.Ln)

        one_minus_up = sb.tile([P, U], F32)
        nc.vector.tensor_scalar(one_minus_up[:], window[:].indirect(up_list[:]), -1.0, 1.0, ALU.mult, ALU.add)
        first, second = pieces(HALVES)
        half_sign = sb.tile([P, HALF], F32)
        nc.vector.tensor_scalar(half_sign[:], inv_sat2[:, second], 1000.0, 0.5, ALU.is_gt, ALU.subtract)
        log_ratio = sb.tile([P, S], F32)
        nc.vector.tensor_tensor(log_ratio[:], log_numerator[:], log_inv_sat2[:], ALU.subtract)
        drive = inv_sat2
        nc.vector.tensor_tensor(drive[:], window[:].indirect(lo_list[:]), one_minus_up[:], ALU.add)

        power = sb.tile([P, S], F32)
        sqrt_term = sb.tile([P, S], F32)
        half_abs = sb.tile([P, HALF], F32)
        signed_power = sb.tile([P, HALF], F32)
        root = sb.tile([P, S], F32)
        nc.scalar.activation(power[:], log_inv_sat2[:], ACT.Exp, scale=-0.125, bias=math.log(4.0))
        for piece in (first, second):
            nc.scalar.activation(sqrt_term[:, piece], log_ratio[:, piece], ACT.Exp, scale=0.5)
        nc.scalar.activation(half_abs[:], sqrt_term[:, first], ACT.Abs, scale=-0.5, bias=0.5)
        nc.vector.tensor_tensor(signed_power[:], half_sign[:], power[:, second], ALU.mult)
        nc.vector.scalar_tensor_tensor(
            root[:, second], sqrt_term[:, second], 1.0, signed_power[:], ALU.subtract, ALU.mult
        )
        nc.vector.tensor_tensor(root[:, first], half_abs[:], power[:, first], ALU.mult)

        up_drive = sb.tile([P, U], F32)
        flux = sb.tile([P, U], F32)
        for piece in pieces(HALVES):
            nc.vector.tensor_tensor(
                up_drive[:, piece], root[:].indirect(up_list[:, list_columns(piece)]), drive[:, piece], ALU.mult
            )
        for piece in pieces(SHORT_END):
            nc.vector.tensor_tensor(
                flux[:, piece], root[:].indirect(lo_list[:, list_columns(piece)]), up_drive[:, piece], ALU.mult
            )
            nc.sync.dma_start(out[:, piece], flux[:, piece])
